import numpy as np
import ml_dtypes


def mxq(x, axis, fmt="e4m3"):
    dtype, down = {"e4m3": (ml_dtypes.float8_e4m3fn, 7), "e5m2": (ml_dtypes.float8_e5m2, 14)}[fmt]
    v = np.moveaxis(np.asarray(x, np.float32).astype(ml_dtypes.bfloat16).astype(np.float64), axis, -1)
    blocks = v.reshape(v.shape[:-1] + (-1, 32))
    amax = np.abs(blocks).max(-1, keepdims=True)
    byte = np.maximum(np.where(amax > 0, np.frexp(amax)[1] - 1 + 127, 0) - down, 1)
    scale = np.exp2(byte - 127.0)
    codes = (blocks / scale).astype(np.float32).astype(dtype).astype(np.float64)
    return np.moveaxis((codes * scale).reshape(v.shape), -1, axis)


WIDE = False


def mx_kscale(k, group=512):
    if not WIDE:
        return np.ones(k)
    levels = np.array([10, -10, 5, -5, 0])
    if group != 512:
        return np.exp2(np.random.permutation(np.resize(levels, k // group))).repeat(group)
    if k % 512:
        return np.exp2(np.random.permutation(np.resize(levels, k // 32))).repeat(32)
    a = np.empty((k // 512, 16))
    for p in range(k // 512):
        a[p, :8] = np.random.permutation(np.resize(levels, 8))
        for g in range(8):
            far = levels[np.abs(levels - a[p, g]) >= 10]
            a[p, g + 8] = far[np.random.randint(len(far))]
    return np.exp2(a.ravel()).repeat(32)


def f64(x):
    return np.asarray(x).astype(np.float64)


E2M1 = np.array([0.0, 0.5, 1.0, 1.5, 2.0, 3.0, 4.0, 6.0, -0.0, -0.5, -1.0, -1.5, -2.0, -3.0, -4.0, -6.0])


def pack_group(w):
    k, n = w.shape
    w = f64(np.asarray(w, np.float32).astype(ml_dtypes.bfloat16)).reshape(k // 32, 32, n)
    amax = np.abs(w).max(1)
    mant, ex = np.frexp(amax / 6.0)
    byte = np.clip(np.where(amax > 0, np.where(mant > 0.5, ex, ex - 1) + 127, 1), 1, 254)
    scaled = (w * np.exp2(127.0 - byte)[:, None, :]).reshape(k, n).astype(np.float32)
    c = np.ascontiguousarray(scaled.reshape(k // 4, 4, n).transpose(0, 2, 1)).astype(ml_dtypes.float4_e2m1fn).view(np.uint8) & 0xF
    return np.ascontiguousarray((c[..., 0::2] | (c[..., 1::2] << 4)).reshape(k // 4, 2 * n)), byte.astype(np.uint8)


def unpack_group(words, scales):
    p, n = words.shape[0], scales.shape[1]
    words = np.ascontiguousarray(words).reshape(p, n, 2)
    nib = np.empty((p, n, 4), np.uint8)
    nib[..., 0::2] = words & 0xF
    nib[..., 1::2] = words >> 4
    return E2M1[nib].transpose(0, 2, 1).reshape(4 * p, n) * np.repeat(np.exp2(scales.astype(np.float64) - 127.0), 32, axis=0)


def gelu(v):
    return 0.5 * v * (1.0 + np.tanh(0.7978845608028654 * (v + 0.044715 * v ** 3)))


G, D, M, N = 2, 256, 128, 512


def setup_inputs():
    n = np.random.standard_normal
    s = mx_kscale(D, 0)[:, None]
    w_ = [pack_group(w) for w in n((G, D, M)) / np.sqrt(D) / s]
    u_ = [pack_group(w) for w in n((G, D, M)) / np.sqrt(D) / s]
    return {
        "x": (n((G, D, N)) * s).astype(np.float32),
        "w_words": np.stack([w[0] for w in w_]),
        "w_scales": np.stack([w[1] for w in w_]),
        "u_words": np.stack([w[0] for w in u_]),
        "u_scales": np.stack([w[1] for w in u_]),
        "b": (0.5 * n((G, M, 1))).astype(np.float32),
        "r": n((G, M, N)).astype(np.float32),
    }


def reference(x, w_words, w_scales, u_words, u_scales, b, r):
    xq = mxq(f64(x), 1, "e4m3")
    h = np.stack([unpack_group(w_words[g], w_scales[g]) for g in range(G)]).transpose(0, 2, 1) @ xq
    g = np.stack([unpack_group(u_words[g], u_scales[g]) for g in range(G)]).transpose(0, 2, 1) @ xq
    h = h + f64(b)
    y = gelu(h) * g
    y = y + f64(r)
    return y

@@ -1,0 +1,130 @@
+from contextlib import ExitStack
+
+import concourse.mybir as mybir
+
+G, D, M, N = 2, 256, 128, 512
+FLOPS = 2 * 2 * G * D * M * N
+
+F32 = mybir.dt.float32
+BF16 = mybir.dt.bfloat16
+I32 = mybir.dt.int32
+U32 = mybir.dt.uint32
+U8 = mybir.dt.uint8
+FP8X4 = mybir.dt.float8_e4m3fn_x4
+FP4X4 = mybir.dt.float4_e2m1fn_x4
+GELU = mybir.ActivationFunctionType.Gelu_apprx_tanh
+ALU = mybir.AluOpType
+
+P = 128
+PACK = 4
+ROWS = D // PACK
+HALF = N // 2
+QW = 128
+VCOLS = 176
+
+
+def tile_rows_gglu_gelu_bias_res_kernel(tc, x, w_words, w_scales, u_words, u_scales, b, r, out):
+    nc = tc.nc
+    x_v = x.rearrange("g (p j) n -> (g p) j n", j=PACK)
+    r_v = r.rearrange("g m n -> m g n")
+    out_v = out.rearrange("g m n -> m g n")
+
+    with ExitStack() as ctx:
+        sb = ctx.enter_context(tc.tile_pool(name="sb", bufs=1))
+        ps = ctx.enter_context(tc.psum_pool(name="ps", bufs=1))
+        ctx.enter_context(tc.manual_schedule())
+
+        raw = [sb.tile([P, PACK, HALF], F32, name="raw%d" % h) for h in range(2)]
+        xb = [sb.tile([P, HALF, PACK], BF16, name="xb%d" % h, align_bytes=64) for h in range(2)]
+        codes = sb.tile([P, N + HALF], U32, name="codes", align_bytes=64)
+        scales = sb.tile([P, N + HALF], U8, name="scales", align_bytes=64)
+        words = [sb.tile([P, 2 * M], U8, name="words%d" % k, align_bytes=64) for k in range(2)]
+        planes = sb.tile([P, 2, M], U8, name="planes", align_bytes=64)
+        bias = sb.tile([P, G, 8], F32, name="bias")
+        res = [sb.tile([P, G, HALF], F32, name="res%d" % h) for h in range(2)]
+        act = [sb.tile([P, G, HALF], F32, name="act%d" % h) for h in range(2)]
+        prod = [sb.tile([P, G, HALF], F32, name="prod%d" % h) for h in range(2)]
+        y = [sb.tile([P, G, HALF], F32, name="y%d" % h) for h in range(2)]
+        warm = sb.tile([P, 16], F32, name="warm")
+        banks = {}
+        for h in range(2):
+            for k in range(2):
+                for g in range(G):
+                    banks[h, k, g] = ps.tile([M, N], F32, name="bank%d%d%d" % (h, k, g))
+
+        def load_scales(eng, k, q):
+            src = (w_scales, u_scales)[k].rearrange("g f m -> (g f) m")
+            eng.dma_start(out=planes[32 * q : 32 * q + 4, k, :].bitcast(I32), in_=src[4 * q : 4 * q + 4, :].bitcast(I32))
+
+        nc.vector.memset(planes[:].rearrange("p k m -> p (k m)").bitcast(I32), 0)
+        nc.vector.memset(warm[:, 0:1], 0.0)
+        nc.vector.memset(scales[:, 0:HALF].bitcast(I32), 0)
+        nc.vector.memset(codes[:, 0:HALF], 0)
+
+        def load_words(eng, k):
+            src = (w_words, u_words)[k].rearrange("g p c -> (g p) c")
+            eng.dma_start(out=words[k][:].bitcast(I32), in_=src.bitcast(I32))
+
+        load_words(nc.scalar, 0)
+        with nc.allow_non_contiguous_dma(reason="one bias a partition"):
+            nc.scalar.dma_start(out=bias[:, :, 0:1], in_=b.rearrange("g m o -> m g o"))
+        for q in range(4):
+            load_scales(nc.scalar, 0, q)
+        for h in range(2):
+            nc.sync.dma_start(out=raw[h][:], in_=x_v[:, :, h * HALF : (h + 1) * HALF])
+        load_words(nc.gpsimd, 1)
+        nc.scalar.activation(out=warm[:, 8:9], in_=warm[:, 0:1], func=GELU)
+        for q in range(4):
+            load_scales(nc.sync, 1, q)
+        for h in range(2):
+            nc.sync.dma_start(out=res[h][:], in_=r_v[:, :, h * HALF : (h + 1) * HALF])
+
+        def interleave(copy, h, c0, c1):
+            copy(out=xb[h][:, c0:c1, :], in_=raw[h][:, :, c0:c1].rearrange("p j n -> p n j"))
+
+        def quantize(h):
+            interleave(nc.scalar.copy, h, VCOLS, HALF)
+            interleave(nc.vector.tensor_copy, h, 0, QW)
+            interleave(nc.vector.tensor_copy, h, QW, VCOLS)
+            for c0 in range(0, HALF, QW):
+                at = (h + 1) * HALF + c0
+                nc.vector.quantize_mx(
+                    out=codes[:, at : at + QW].bitcast(FP8X4),
+                    scales=scales[:, at : at + QW],
+                    in_=xb[h][:, c0 : c0 + QW, :].rearrange("p n j -> p (n j)"),
+                )
+
+        def multiply(h):
+            cols = slice(h * HALF, h * HALF + N)
+            for k in range(2):
+                for g in range(G):
+                    rows = slice(ROWS * g, ROWS * (g + 1))
+                    nc.tensor.matmul_mx(
+                        out=banks[h, k, g][:],
+                        lhsT=words[k][rows, :].bitcast(FP4X4),
+                        lhsT_scale=planes[rows, k, :],
+                        rhs=codes[rows, cols].bitcast(FP8X4),
+                        rhs_scale=scales[rows, cols],
+                        start=True,
+                        stop=True,
+                    )
+
+        def gelu(h):
+            for g in range(G):
+                nc.scalar.activation(out=act[h][:, g, :], in_=banks[h, 0, g][:, HALF:N], func=GELU, bias=bias[:, g, 0:1])
+
+        def finish(h):
+            for g in range(G):
+                nc.vector.tensor_tensor(out=prod[h][:, g, :], in0=banks[h, 1, g][:, HALF:N], in1=act[h][:, g, :], op=ALU.mult)
+            for g in range(G):
+                nc.vector.tensor_tensor(out=y[h][:, g, :], in0=prod[h][:, g, :], in1=res[h][:, g, :], op=ALU.add)
+                nc.sync.dma_start(out=out_v[:, g, h * HALF : (h + 1) * HALF], in_=y[h][:, g, :])
+
+        quantize(0)
+        multiply(0)
+        quantize(1)
+        multiply(1)
+        gelu(0)
+        finish(0)
+        gelu(1)
+        finish(1)

@@ -20,111 +20,120 @@ PACK = 4
 ROWS = D // PACK
 HALF = N // 2
 QW = 128
-VCOLS = 176
+CHUNKS = ((0, 256), (256, 384), (384, 512))
+EARLY = 256
+PAD = N - EARLY
 
 
 def tile_rows_gglu_gelu_bias_res_kernel(tc, x, w_words, w_scales, u_words, u_scales, b, r, out):
     nc = tc.nc
     x_v = x.rearrange("g (p j) n -> (g p) j n", j=PACK)
-    r_v = r.rearrange("g m n -> m g n")
-    out_v = out.rearrange("g m n -> m g n")
 
     with ExitStack() as ctx:
         sb = ctx.enter_context(tc.tile_pool(name="sb", bufs=1))
         ps = ctx.enter_context(tc.psum_pool(name="ps", bufs=1))
         ctx.enter_context(tc.manual_schedule())
 
-        raw = [sb.tile([P, PACK, HALF], F32, name="raw%d" % h) for h in range(2)]
-        xb = [sb.tile([P, HALF, PACK], BF16, name="xb%d" % h, align_bytes=64) for h in range(2)]
-        codes = sb.tile([P, N + HALF], U32, name="codes", align_bytes=64)
-        scales = sb.tile([P, N + HALF], U8, name="scales", align_bytes=64)
+        raw = [sb.tile([P, PACK, c1 - c0], F32, name="raw%d" % c0) for c0, c1 in CHUNKS]
+        xb = sb.tile([P, N, PACK], BF16, name="xb", align_bytes=64)
+        codes = sb.tile([P, PAD + N], U32, name="codes", align_bytes=64)
+        scales = sb.tile([P, PAD + N], U8, name="scales", align_bytes=64)
         words = [sb.tile([P, 2 * M], U8, name="words%d" % k, align_bytes=64) for k in range(2)]
         planes = sb.tile([P, 2, M], U8, name="planes", align_bytes=64)
         bias = sb.tile([P, G, 8], F32, name="bias")
-        res = [sb.tile([P, G, HALF], F32, name="res%d" % h) for h in range(2)]
-        act = [sb.tile([P, G, HALF], F32, name="act%d" % h) for h in range(2)]
-        prod = [sb.tile([P, G, HALF], F32, name="prod%d" % h) for h in range(2)]
-        y = [sb.tile([P, G, HALF], F32, name="y%d" % h) for h in range(2)]
+        res = [sb.tile([P, N], F32, name="res%d" % g) for g in range(G)]
+        act = [sb.tile([P, N], F32, name="act%d" % g) for g in range(G)]
+        prod = [sb.tile([P, N], F32, name="prod%d" % g) for g in range(G)]
+        y = [sb.tile([P, N], F32, name="y%d" % g) for g in range(G)]
         warm = sb.tile([P, 16], F32, name="warm")
         banks = {}
-        for h in range(2):
-            for k in range(2):
-                for g in range(G):
-                    banks[h, k, g] = ps.tile([M, N], F32, name="bank%d%d%d" % (h, k, g))
+        for k in range(2):
+            for g in range(G):
+                banks[k, g] = ps.tile([M, N], F32, name="bank%d%d" % (k, g))
+        early = [ps.tile([M, N], F32, name="early%d" % k) for k in range(2)]
 
-        def load_scales(eng, k, q):
+        def load_scales(k, q):
             src = (w_scales, u_scales)[k].rearrange("g f m -> (g f) m")
-            eng.dma_start(out=planes[32 * q : 32 * q + 4, k, :].bitcast(I32), in_=src[4 * q : 4 * q + 4, :].bitcast(I32))
-
-        nc.vector.memset(planes[:].rearrange("p k m -> p (k m)").bitcast(I32), 0)
-        nc.vector.memset(warm[:, 0:1], 0.0)
-        nc.vector.memset(scales[:, 0:HALF].bitcast(I32), 0)
-        nc.vector.memset(codes[:, 0:HALF], 0)
+            nc.sync.dma_start(out=planes[32 * q : 32 * q + 4, k, :].bitcast(I32), in_=src[4 * q : 4 * q + 4, :].bitcast(I32))
 
         def load_words(eng, k):
             src = (w_words, u_words)[k].rearrange("g p c -> (g p) c")
             eng.dma_start(out=words[k][:].bitcast(I32), in_=src.bitcast(I32))
 
-        load_words(nc.scalar, 0)
-        with nc.allow_non_contiguous_dma(reason="one bias a partition"):
-            nc.scalar.dma_start(out=bias[:, :, 0:1], in_=b.rearrange("g m o -> m g o"))
-        for q in range(4):
-            load_scales(nc.scalar, 0, q)
-        for h in range(2):
-            nc.sync.dma_start(out=raw[h][:], in_=x_v[:, :, h * HALF : (h + 1) * HALF])
+        nc.vector.memset(planes[:].rearrange("p k m -> p (k m)").bitcast(I32), 0)
+        nc.vector.memset(warm[:, 0:1], 0.0)
+        nc.vector.memset(scales[:, 0:PAD].bitcast(I32), 0)
+        nc.vector.memset(codes[:, 0:PAD], 0)
+
+        def load_x(i):
+            nc.sync.dma_start(out=raw[i][:], in_=x_v[:, :, CHUNKS[i][0] : CHUNKS[i][1]])
+
+        load_x(0)
+        load_words(nc.sync, 0)
+        for k in range(2):
+            for q in (2, 3):
+                load_scales(k, q)
+            if k == 0:
+                load_x(1)
+        load_x(2)
+        for k in range(2):
+            for q in (0, 1):
+                load_scales(k, q)
         load_words(nc.gpsimd, 1)
+        with nc.allow_non_contiguous_dma(reason="one bias a partition"):
+            nc.gpsimd.dma_start(out=bias[:, :, 0:1], in_=b.rearrange("g m o -> m g o"))
+        for g in (1, 0):
+            nc.sync.dma_start(out=res[g][:], in_=r[g])
         nc.scalar.activation(out=warm[:, 8:9], in_=warm[:, 0:1], func=GELU)
-        for q in range(4):
-            load_scales(nc.sync, 1, q)
-        for h in range(2):
-            nc.sync.dma_start(out=res[h][:], in_=r_v[:, :, h * HALF : (h + 1) * HALF])
 
-        def interleave(copy, h, c0, c1):
-            copy(out=xb[h][:, c0:c1, :], in_=raw[h][:, :, c0:c1].rearrange("p j n -> p n j"))
+        def interleave(copy, i, c0, c1):
+            first = CHUNKS[i][0]
+            copy(out=xb[:, c0:c1, :], in_=raw[i][:, :, c0 - first : c1 - first].rearrange("p j n -> p n j"))
 
-        def quantize(h):
-            interleave(nc.scalar.copy, h, VCOLS, HALF)
-            interleave(nc.vector.tensor_copy, h, 0, QW)
-            interleave(nc.vector.tensor_copy, h, QW, VCOLS)
-            for c0 in range(0, HALF, QW):
-                at = (h + 1) * HALF + c0
-                nc.vector.quantize_mx(
-                    out=codes[:, at : at + QW].bitcast(FP8X4),
-                    scales=scales[:, at : at + QW],
-                    in_=xb[h][:, c0 : c0 + QW, :].rearrange("p n j -> p (n j)"),
-                )
+        def quantize(c0):
+            nc.vector.quantize_mx(
+                out=codes[:, PAD + c0 : PAD + c0 + QW].bitcast(FP8X4),
+                scales=scales[:, PAD + c0 : PAD + c0 + QW],
+                in_=xb[:, c0 : c0 + QW, :].rearrange("p n j -> p (n j)"),
+            )
 
-        def multiply(h):
-            cols = slice(h * HALF, h * HALF + N)
-            for k in range(2):
-                for g in range(G):
-                    rows = slice(ROWS * g, ROWS * (g + 1))
-                    nc.tensor.matmul_mx(
-                        out=banks[h, k, g][:],
-                        lhsT=words[k][rows, :].bitcast(FP4X4),
-                        lhsT_scale=planes[rows, k, :],
-                        rhs=codes[rows, cols].bitcast(FP8X4),
-                        rhs_scale=scales[rows, cols],
-                        start=True,
-                        stop=True,
-                    )
+        def multiply(bank, k, g, first):
+            rows = slice(ROWS * g, ROWS * (g + 1))
+            nc.tensor.matmul_mx(
+                out=bank[:],
+                lhsT=words[k][rows, :].bitcast(FP4X4),
+                lhsT_scale=planes[rows, k, :],
+                rhs=codes[rows, first : first + N].bitcast(FP8X4),
+                rhs_scale=scales[rows, first : first + N],
+                start=True,
+                stop=True,
+            )
 
-        def gelu(h):
-            for g in range(G):
-                nc.scalar.activation(out=act[h][:, g, :], in_=banks[h, 0, g][:, HALF:N], func=GELU, bias=bias[:, g, 0:1])
+        def finish(h_bank, u_bank, g, pieces, shift):
+            for c0, c1 in pieces:
+                nc.scalar.activation(out=act[g][:, c0:c1], in_=h_bank[:, shift + c0 : shift + c1], func=GELU, bias=bias[:, g, 0:1])
+            for c0, c1 in pieces:
+                nc.vector.tensor_tensor(out=prod[g][:, c0:c1], in0=u_bank[:, shift + c0 : shift + c1], in1=act[g][:, c0:c1], op=ALU.mult)
+            for c0, c1 in pieces:
+                nc.vector.tensor_tensor(out=y[g][:, c0:c1], in0=prod[g][:, c0:c1], in1=res[g][:, c0:c1], op=ALU.add)
+                nc.sync.dma_start(out=out[g][:, c0:c1], in_=y[g][:, c0:c1])
 
-        def finish(h):
-            for g in range(G):
-                nc.vector.tensor_tensor(out=prod[h][:, g, :], in0=banks[h, 1, g][:, HALF:N], in1=act[h][:, g, :], op=ALU.mult)
-            for g in range(G):
-                nc.vector.tensor_tensor(out=y[h][:, g, :], in0=prod[h][:, g, :], in1=res[h][:, g, :], op=ALU.add)
-                nc.sync.dma_start(out=out_v[:, g, h * HALF : (h + 1) * HALF], in_=y[h][:, g, :])
-
+        interleave(nc.scalar.copy, 0, 160, 256)
+        interleave(nc.vector.tensor_copy, 0, 0, 128)
+        interleave(nc.vector.tensor_copy, 0, 128, 160)
         quantize(0)
-        multiply(0)
-        quantize(1)
-        multiply(1)
-        gelu(0)
-        finish(0)
-        gelu(1)
-        finish(1)
+        quantize(128)
+        for k in range(2):
+            multiply(early[k], k, 1, 0)
+        interleave(nc.scalar.copy, 1, 328, 384)
+        interleave(nc.vector.tensor_copy, 1, 256, 328)
+        interleave(nc.scalar.copy, 2, 448, 512)
+        interleave(nc.vector.tensor_copy, 2, 384, 448)
+        quantize(256)
+        quantize(384)
+        for g in range(G):
+            for k in range(2):
+                multiply(banks[k, g], k, g, PAD)
+        finish(early[0], early[1], 1, [(0, 256)], PAD)
+        finish(banks[0, 0], banks[1, 0], 0, [(0, 256), (256, 512)], 0)
+        finish(banks[0, 1], banks[1, 1], 1, [(256, 384), (384, 512)], 0)

@@ -16,124 +16,135 @@ GELU = mybir.ActivationFunctionType.Gelu_apprx_tanh
 ALU = mybir.AluOpType
 
 P = 128
+QUAD = 32
+SCALE_ROWS = 4
 PACK = 4
 ROWS = D // PACK
 HALF = N // 2
-QW = 128
-CHUNKS = ((0, 256), (256, 384), (384, 512))
-EARLY = 256
-PAD = N - EARLY
+QUARTER = N // 4
+SCALAR_COLS = 96
+W, U = 0, 1
+EARLY_GROUP, LATE_GROUP = 1, 0
 
 
 def tile_rows_gglu_gelu_bias_res_kernel(tc, x, w_words, w_scales, u_words, u_scales, b, r, out):
     nc = tc.nc
-    x_v = x.rearrange("g (p j) n -> (g p) j n", j=PACK)
+    x_rows = x.rearrange("g (p j) n -> (g p) j n", j=PACK)
 
     with ExitStack() as ctx:
         sb = ctx.enter_context(tc.tile_pool(name="sb", bufs=1))
         ps = ctx.enter_context(tc.psum_pool(name="ps", bufs=1))
         ctx.enter_context(tc.manual_schedule())
 
-        raw = [sb.tile([P, PACK, c1 - c0], F32, name="raw%d" % c0) for c0, c1 in CHUNKS]
+        raw = [sb.tile([P, PACK, HALF], F32, name="raw%d" % h) for h in range(2)]
         xb = sb.tile([P, N, PACK], BF16, name="xb", align_bytes=64)
-        codes = sb.tile([P, PAD + N], U32, name="codes", align_bytes=64)
-        scales = sb.tile([P, PAD + N], U8, name="scales", align_bytes=64)
-        words = [sb.tile([P, 2 * M], U8, name="words%d" % k, align_bytes=64) for k in range(2)]
-        planes = sb.tile([P, 2, M], U8, name="planes", align_bytes=64)
-        bias = sb.tile([P, G, 8], F32, name="bias")
+        codes = sb.tile([P, HALF + N], U32, name="codes", align_bytes=64)
+        scales = sb.tile([P, HALF + N], U8, name="scales", align_bytes=64)
+        words = [sb.tile([P, 2 * M], U8, name="words%d" % k, align_bytes=64) for k in (W, U)]
+        weight_scales = sb.tile([P, 2, M], U8, name="weight_scales", align_bytes=64)
+        bias_rows = sb.tile([P, G, QUAD], F32, name="bias_rows", align_bytes=64)
+        bias = sb.tile([P, G, QUAD], F32, name="bias", align_bytes=64)
         res = [sb.tile([P, N], F32, name="res%d" % g) for g in range(G)]
         act = [sb.tile([P, N], F32, name="act%d" % g) for g in range(G)]
         prod = [sb.tile([P, N], F32, name="prod%d" % g) for g in range(G)]
         y = [sb.tile([P, N], F32, name="y%d" % g) for g in range(G)]
         warm = sb.tile([P, 16], F32, name="warm")
         banks = {}
-        for k in range(2):
+        for k in (W, U):
             for g in range(G):
                 banks[k, g] = ps.tile([M, N], F32, name="bank%d%d" % (k, g))
-        early = [ps.tile([M, N], F32, name="early%d" % k) for k in range(2)]
+        early_banks = [ps.tile([M, N], F32, name="early%d" % k) for k in (W, U)]
 
-        def load_scales(k, q):
-            src = (w_scales, u_scales)[k].rearrange("g f m -> (g f) m")
-            nc.sync.dma_start(out=planes[32 * q : 32 * q + 4, k, :].bitcast(I32), in_=src[4 * q : 4 * q + 4, :].bitcast(I32))
+        def load_x(h):
+            nc.sync.dma_start(out=raw[h][:], in_=x_rows[:, :, h * HALF : (h + 1) * HALF])
 
-        def load_words(eng, k):
+        def load_words(k):
             src = (w_words, u_words)[k].rearrange("g p c -> (g p) c")
-            eng.dma_start(out=words[k][:].bitcast(I32), in_=src.bitcast(I32))
+            nc.sync.dma_start(out=words[k][:].bitcast(I32), in_=src.bitcast(I32))
 
-        nc.vector.memset(planes[:].rearrange("p k m -> p (k m)").bitcast(I32), 0)
-        nc.vector.memset(warm[:, 0:1], 0.0)
-        nc.vector.memset(scales[:, 0:PAD].bitcast(I32), 0)
-        nc.vector.memset(codes[:, 0:PAD], 0)
+        def load_weight_scales(k, g):
+            src = (w_scales, u_scales)[k].rearrange("g f m -> (g f) m")
+            for q in (2 * g, 2 * g + 1):
+                nc.sync.dma_start(
+                    out=weight_scales[QUAD * q : QUAD * q + SCALE_ROWS, k, :].bitcast(I32),
+                    in_=src[SCALE_ROWS * q : SCALE_ROWS * (q + 1), :].bitcast(I32),
+                )
 
-        def load_x(i):
-            nc.sync.dma_start(out=raw[i][:], in_=x_v[:, :, CHUNKS[i][0] : CHUNKS[i][1]])
+        def interleave(copy, c0, c1):
+            h, first = c0 // HALF, c0 % HALF
+            copy(out=xb[:, c0:c1, :], in_=raw[h][:, :, first : first + c1 - c0].rearrange("p j n -> p n j"))
 
-        load_x(0)
-        load_words(nc.sync, 0)
-        for k in range(2):
-            for q in (2, 3):
-                load_scales(k, q)
-            if k == 0:
-                load_x(1)
-        load_x(2)
-        for k in range(2):
-            for q in (0, 1):
-                load_scales(k, q)
-        load_words(nc.gpsimd, 1)
-        with nc.allow_non_contiguous_dma(reason="one bias a partition"):
-            nc.gpsimd.dma_start(out=bias[:, :, 0:1], in_=b.rearrange("g m o -> m g o"))
-        for g in (1, 0):
-            nc.sync.dma_start(out=res[g][:], in_=r[g])
-        nc.scalar.activation(out=warm[:, 8:9], in_=warm[:, 0:1], func=GELU)
-
-        def interleave(copy, i, c0, c1):
-            first = CHUNKS[i][0]
-            copy(out=xb[:, c0:c1, :], in_=raw[i][:, :, c0 - first : c1 - first].rearrange("p j n -> p n j"))
-
-        def quantize(c0):
-            nc.vector.quantize_mx(
-                out=codes[:, PAD + c0 : PAD + c0 + QW].bitcast(FP8X4),
-                scales=scales[:, PAD + c0 : PAD + c0 + QW],
-                in_=xb[:, c0 : c0 + QW, :].rearrange("p n j -> p (n j)"),
-            )
+        def quantize_half(h):
+            c0 = h * HALF
+            split = c0 + HALF - SCALAR_COLS
+            interleave(nc.scalar.copy, split, c0 + HALF)
+            interleave(nc.vector.tensor_copy, c0, c0 + QUARTER)
+            interleave(nc.vector.tensor_copy, c0 + QUARTER, split)
+            for c in (c0, c0 + QUARTER):
+                nc.vector.quantize_mx(
+                    out=codes[:, HALF + c : HALF + c + QUARTER].bitcast(FP8X4),
+                    scales=scales[:, HALF + c : HALF + c + QUARTER],
+                    in_=xb[:, c : c + QUARTER, :].rearrange("p n j -> p (n j)"),
+                )
 
         def multiply(bank, k, g, first):
             rows = slice(ROWS * g, ROWS * (g + 1))
             nc.tensor.matmul_mx(
                 out=bank[:],
                 lhsT=words[k][rows, :].bitcast(FP4X4),
-                lhsT_scale=planes[rows, k, :],
+                lhsT_scale=weight_scales[rows, k, :],
                 rhs=codes[rows, first : first + N].bitcast(FP8X4),
                 rhs_scale=scales[rows, first : first + N],
                 start=True,
                 stop=True,
             )
 
-        def finish(h_bank, u_bank, g, pieces, shift):
-            for c0, c1 in pieces:
-                nc.scalar.activation(out=act[g][:, c0:c1], in_=h_bank[:, shift + c0 : shift + c1], func=GELU, bias=bias[:, g, 0:1])
-            for c0, c1 in pieces:
-                nc.vector.tensor_tensor(out=prod[g][:, c0:c1], in0=u_bank[:, shift + c0 : shift + c1], in1=act[g][:, c0:c1], op=ALU.mult)
-            for c0, c1 in pieces:
-                nc.vector.tensor_tensor(out=y[g][:, c0:c1], in0=prod[g][:, c0:c1], in1=res[g][:, c0:c1], op=ALU.add)
-                nc.sync.dma_start(out=out[g][:, c0:c1], in_=y[g][:, c0:c1])
+        def finish(w_bank, u_bank, g, starts, width, shift):
+            for c in starts:
+                nc.scalar.activation(
+                    out=act[g][:, c : c + width], in_=w_bank[:, shift + c : shift + c + width], func=GELU, bias=bias[:, g, 0:1]
+                )
+            for c in starts:
+                nc.vector.tensor_tensor(
+                    out=prod[g][:, c : c + width],
+                    in0=u_bank[:, shift + c : shift + c + width],
+                    in1=act[g][:, c : c + width],
+                    op=ALU.mult,
+                )
+            for c in starts:
+                cols = slice(c, c + width)
+                nc.vector.tensor_tensor(out=y[g][:, cols], in0=prod[g][:, cols], in1=res[g][:, cols], op=ALU.add)
+                nc.sync.dma_start(out=out[g][:, cols], in_=y[g][:, cols])
 
-        interleave(nc.scalar.copy, 0, 160, 256)
-        interleave(nc.vector.tensor_copy, 0, 0, 128)
-        interleave(nc.vector.tensor_copy, 0, 128, 160)
-        quantize(0)
-        quantize(128)
-        for k in range(2):
-            multiply(early[k], k, 1, 0)
-        interleave(nc.scalar.copy, 1, 328, 384)
-        interleave(nc.vector.tensor_copy, 1, 256, 328)
-        interleave(nc.scalar.copy, 2, 448, 512)
-        interleave(nc.vector.tensor_copy, 2, 384, 448)
-        quantize(256)
-        quantize(384)
-        for g in range(G):
-            for k in range(2):
-                multiply(banks[k, g], k, g, PAD)
-        finish(early[0], early[1], 1, [(0, 256)], PAD)
-        finish(banks[0, 0], banks[1, 0], 0, [(0, 256), (256, 512)], 0)
-        finish(banks[0, 1], banks[1, 1], 1, [(256, 384), (384, 512)], 0)
+        nc.vector.memset(weight_scales[:].rearrange("p k m -> p (k m)").bitcast(I32), 0)
+        nc.vector.memset(bias_rows[:], 0.0)
+        nc.vector.memset(warm[:, 0:1], 0.0)
+        nc.vector.memset(scales[:, 0:HALF].bitcast(I32), 0)
+        nc.vector.memset(codes[:, 0:HALF], 0)
+
+        load_x(0)
+        for k in (W, U):
+            load_words(k)
+        for k in (W, U):
+            load_weight_scales(k, EARLY_GROUP)
+        load_x(1)
+        load_weight_scales(W, LATE_GROUP)
+        nc.sync.dma_start(out=bias_rows[0:P:QUAD, :, :], in_=b.rearrange("g (q i) o -> q g (i o)", i=QUAD))
+        load_weight_scales(U, LATE_GROUP)
+        for g in (EARLY_GROUP, LATE_GROUP):
+            nc.sync.dma_start(out=res[g][:], in_=r[g])
+        nc.scalar.activation(out=warm[:, 8:9], in_=warm[:, 0:1], func=GELU)
+
+        quantize_half(0)
+        for k in (W, U):
+            multiply(early_banks[k], k, EARLY_GROUP, 0)
+        quantize_half(1)
+        for g in (EARLY_GROUP, LATE_GROUP):
+            nc.vector.transpose(out=bias[:, g, :], in_=bias_rows[:, g, :])
+        for g in (LATE_GROUP, EARLY_GROUP):
+            for k in (W, U):
+                multiply(banks[k, g], k, g, HALF)
+
+        finish(early_banks[W], early_banks[U], EARLY_GROUP, (0,), HALF, HALF)
+        finish(banks[W, LATE_GROUP], banks[U, LATE_GROUP], LATE_GROUP, (0, HALF), HALF, 0)
+        finish(banks[W, EARLY_GROUP], banks[U, EARLY_GROUP], EARLY_GROUP, (HALF, HALF + QUARTER), QUARTER, 0)

from contextlib import ExitStack

import concourse.mybir as mybir

G, D, M, N = 2, 256, 128, 512
FLOPS = 2 * 2 * G * D * M * N

F32 = mybir.dt.float32
BF16 = mybir.dt.bfloat16
I32 = mybir.dt.int32
U32 = mybir.dt.uint32
U8 = mybir.dt.uint8
FP8X4 = mybir.dt.float8_e4m3fn_x4
FP4X4 = mybir.dt.float4_e2m1fn_x4
GELU = mybir.ActivationFunctionType.Gelu_apprx_tanh
ALU = mybir.AluOpType

P = 128
QUAD = 32
SCALE_ROWS = 4
PACK = 4
ROWS = D // PACK
HALF = N // 2
QUARTER = N // 4
SCALAR_COLS = 96
W, U = 0, 1
EARLY_GROUP, LATE_GROUP = 1, 0


def tile_rows_gglu_gelu_bias_res_kernel(tc, x, w_words, w_scales, u_words, u_scales, b, r, out):
    nc = tc.nc
    x_rows = x.rearrange("g (p j) n -> (g p) j n", j=PACK)

    with ExitStack() as ctx:
        sb = ctx.enter_context(tc.tile_pool(name="sb", bufs=1))
        ps = ctx.enter_context(tc.psum_pool(name="ps", bufs=1))
        ctx.enter_context(tc.manual_schedule())

        raw = [sb.tile([P, PACK, HALF], F32, name="raw%d" % h) for h in range(2)]
        xb = sb.tile([P, N, PACK], BF16, name="xb", align_bytes=64)
        codes = sb.tile([P, HALF + N], U32, name="codes", align_bytes=64)
        scales = sb.tile([P, HALF + N], U8, name="scales", align_bytes=64)
        words = [sb.tile([P, 2 * M], U8, name="words%d" % k, align_bytes=64) for k in (W, U)]
        weight_scales = sb.tile([P, 2, M], U8, name="weight_scales", align_bytes=64)
        bias_rows = sb.tile([P, G, QUAD], F32, name="bias_rows", align_bytes=64)
        bias = sb.tile([P, G, QUAD], F32, name="bias", align_bytes=64)
        res = [sb.tile([P, N], F32, name="res%d" % g) for g in range(G)]
        act = [sb.tile([P, N], F32, name="act%d" % g) for g in range(G)]
        prod = [sb.tile([P, N], F32, name="prod%d" % g) for g in range(G)]
        y = [sb.tile([P, N], F32, name="y%d" % g) for g in range(G)]
        warm = sb.tile([P, 16], F32, name="warm")
        banks = {}
        for k in (W, U):
            for g in range(G):
                banks[k, g] = ps.tile([M, N], F32, name="bank%d%d" % (k, g))
        early_banks = [ps.tile([M, N], F32, name="early%d" % k) for k in (W, U)]

        def load_x(h):
            nc.sync.dma_start(out=raw[h][:], in_=x_rows[:, :, h * HALF : (h + 1) * HALF])

        def load_words(k):
            src = (w_words, u_words)[k].rearrange("g p c -> (g p) c")
            nc.sync.dma_start(out=words[k][:].bitcast(I32), in_=src.bitcast(I32))

        def load_weight_scales(k, g):
            src = (w_scales, u_scales)[k].rearrange("g f m -> (g f) m")
            for q in (2 * g, 2 * g + 1):
                nc.sync.dma_start(
                    out=weight_scales[QUAD * q : QUAD * q + SCALE_ROWS, k, :].bitcast(I32),
                    in_=src[SCALE_ROWS * q : SCALE_ROWS * (q + 1), :].bitcast(I32),
                )

        def interleave(copy, c0, c1):
            h, first = c0 // HALF, c0 % HALF
            copy(out=xb[:, c0:c1, :], in_=raw[h][:, :, first : first + c1 - c0].rearrange("p j n -> p n j"))

        def quantize_half(h):
            c0 = h * HALF
            split = c0 + HALF - SCALAR_COLS
            interleave(nc.scalar.copy, split, c0 + HALF)
            interleave(nc.vector.tensor_copy, c0, c0 + QUARTER)
            interleave(nc.vector.tensor_copy, c0 + QUARTER, split)
            for c in (c0, c0 + QUARTER):
                nc.vector.quantize_mx(
                    out=codes[:, HALF + c : HALF + c + QUARTER].bitcast(FP8X4),
                    scales=scales[:, HALF + c : HALF + c + QUARTER],
                    in_=xb[:, c : c + QUARTER, :].rearrange("p n j -> p (n j)"),
                )

        def multiply(bank, k, g, first):
            rows = slice(ROWS * g, ROWS * (g + 1))
            nc.tensor.matmul_mx(
                out=bank[:],
                lhsT=words[k][rows, :].bitcast(FP4X4),
                lhsT_scale=weight_scales[rows, k, :],
                rhs=codes[rows, first : first + N].bitcast(FP8X4),
                rhs_scale=scales[rows, first : first + N],
                start=True,
                stop=True,
            )

        def finish(w_bank, u_bank, g, starts, width, shift):
            for c in starts:
                nc.scalar.activation(
                    out=act[g][:, c : c + width], in_=w_bank[:, shift + c : shift + c + width], func=GELU, bias=bias[:, g, 0:1]
                )
            for c in starts:
                nc.vector.tensor_tensor(
                    out=prod[g][:, c : c + width],
                    in0=u_bank[:, shift + c : shift + c + width],
                    in1=act[g][:, c : c + width],
                    op=ALU.mult,
                )
            for c in starts:
                cols = slice(c, c + width)
                nc.vector.tensor_tensor(out=y[g][:, cols], in0=prod[g][:, cols], in1=res[g][:, cols], op=ALU.add)
                nc.sync.dma_start(out=out[g][:, cols], in_=y[g][:, cols])

        nc.vector.memset(weight_scales[:].rearrange("p k m -> p (k m)").bitcast(I32), 0)
        nc.vector.memset(bias_rows[:], 0.0)
        nc.vector.memset(warm[:, 0:1], 0.0)
        nc.vector.memset(scales[:, 0:HALF].bitcast(I32), 0)
        nc.vector.memset(codes[:, 0:HALF], 0)

        load_x(0)
        for k in (W, U):
            load_words(k)
        for k in (W, U):
            load_weight_scales(k, EARLY_GROUP)
        load_x(1)
        load_weight_scales(W, LATE_GROUP)
        nc.sync.dma_start(out=bias_rows[0:P:QUAD, :, :], in_=b.rearrange("g (q i) o -> q g (i o)", i=QUAD))
        load_weight_scales(U, LATE_GROUP)
        for g in (EARLY_GROUP, LATE_GROUP):
            nc.sync.dma_start(out=res[g][:], in_=r[g])
        nc.scalar.activation(out=warm[:, 8:9], in_=warm[:, 0:1], func=GELU)

        quantize_half(0)
        for k in (W, U):
            multiply(early_banks[k], k, EARLY_GROUP, 0)
        quantize_half(1)
        for g in (EARLY_GROUP, LATE_GROUP):
            nc.vector.transpose(out=bias[:, g, :], in_=bias_rows[:, g, :])
        for g in (LATE_GROUP, EARLY_GROUP):
            for k in (W, U):
                multiply(banks[k, g], k, g, HALF)

        finish(early_banks[W], early_banks[U], EARLY_GROUP, (0,), HALF, HALF)
        finish(banks[W, LATE_GROUP], banks[U, LATE_GROUP], LATE_GROUP, (0, HALF), HALF, 0)
        finish(banks[W, EARLY_GROUP], banks[U, EARLY_GROUP], EARLY_GROUP, (HALF, HALF + QUARTER), QUARTER, 0)
